import numpy as np
import ml_dtypes


def mxq(x, axis, fmt="e4m3"):
    dtype, down = {"e4m3": (ml_dtypes.float8_e4m3fn, 7), "e5m2": (ml_dtypes.float8_e5m2, 14)}[fmt]
    v = np.moveaxis(np.asarray(x, np.float32).astype(ml_dtypes.bfloat16).astype(np.float64), axis, -1)
    blocks = v.reshape(v.shape[:-1] + (-1, 32))
    amax = np.abs(blocks).max(-1, keepdims=True)
    byte = np.maximum(np.where(amax > 0, np.frexp(amax)[1] - 1 + 127, 0) - down, 1)
    scale = np.exp2(byte - 127.0)
    codes = (blocks / scale).astype(np.float32).astype(dtype).astype(np.float64)
    return np.moveaxis((codes * scale).reshape(v.shape), -1, axis)


WIDE = False


def mx_kscale(k):
    if not WIDE:
        return np.ones(k)
    levels = np.array([10, -10, 5, -5, 0])
    if k % 512:
        return np.exp2(np.random.permutation(np.resize(levels, k // 32))).repeat(32)
    a = np.empty((k // 512, 16))
    for p in range(k // 512):
        a[p, :8] = np.random.permutation(np.resize(levels, 8))
        for g in range(8):
            far = levels[np.abs(levels - a[p, g]) >= 10]
            a[p, g + 8] = far[np.random.randint(len(far))]
    return np.exp2(a.ravel()).repeat(32)


def f64(x):
    return np.asarray(x).astype(np.float64)


def striped(idx):
    return np.tile(idx.reshape(-1, 16).T, (8, 1)).astype(np.uint16)


def unstriped(offs):
    return offs[:16].T.reshape(-1).astype(np.int64)

def planes(y):
    n, m = y.shape
    v = y.astype(np.float32).astype(ml_dtypes.bfloat16).astype(np.float64).reshape(n // 32, 32, m)
    top = np.abs(v).max(1)
    byte = np.clip(np.where(top > 0, np.frexp(top)[1] - 1 + 127 - 7, 1), 1, 254)
    codes = (v * np.exp2(127.0 - byte)[:, None, :]).reshape(n, m).astype(np.float32).astype(ml_dtypes.float8_e4m3fn).view(np.uint8)
    words = codes.reshape(n // 512, 128, 4, m).transpose(0, 1, 3, 2)
    return np.ascontiguousarray(words), np.ascontiguousarray(byte.astype(np.uint8).reshape(n // 512, 16, m))


K, T, S, N = 512, 1024, 512, 512


def setup_inputs():
    n = np.random.standard_normal
    s = mx_kscale(K)[:, None]
    return {
        "xT": (n((K, T)) * s).astype(np.float32),
        "w1": (n((K, N)) / np.sqrt(K) / s).astype(np.float32),
        "offs": striped(np.random.permutation(T)[:S]),
    }


def reference(xT, w1, offs):
    xq = mxq(f64(xT)[:, unstriped(offs)], 0, "e4m3")
    y = mxq(f64(w1), 0, "e4m3").T @ xq
    e = np.exp(y - y.max(axis=1, keepdims=True))
    out_0 = e / e.sum(axis=1, keepdims=True)
    return (out_0,) + planes(out_0)

@@ -1,0 +1,121 @@
+from contextlib import ExitStack
+
+import concourse.mybir as mybir
+
+K, T, S, N = 512, 1024, 512, 512
+FLOPS = 2 * K * S * N
+
+F32 = mybir.dt.float32
+BF16 = mybir.dt.bfloat16
+I32 = mybir.dt.int32
+U32 = mybir.dt.uint32
+U16 = mybir.dt.uint16
+U8 = mybir.dt.uint8
+FP8X4 = mybir.dt.float8_e4m3fn_x4
+ACT = mybir.ActivationFunctionType
+ALU = mybir.AluOpType
+AXIS = mybir.AxisListType
+
+P = 128
+PACK = 4
+RUN = 4
+HALF = S // 2
+W_SPLIT = 44
+O_SPLIT = 336
+
+
+def tile_picked_rank_none_lo_kernel(tc, xT, w1, offs, out_0, out_1, out_2):
+    nc = tc.nc
+    with ExitStack() as ctx:
+        keep = ctx.enter_context(tc.tile_pool(name="keep", bufs=1))
+        psum = ctx.enter_context(tc.psum_pool(name="psum", bufs=1))
+
+        offsets = keep.tile([P, S // 16], U16, name="offsets")
+        nc.sync.dma_start(offsets[:], offs)
+
+        x_rows = xT.rearrange("(p j) c -> p j c", j=PACK)
+        x_plane = [keep.tile([P, T], F32, name="x_plane%d" % j) for j in range(PACK)]
+        for j in range(PACK):
+            nc.sync.dma_start(x_plane[j][:], x_rows[:, j, :])
+        w_rows = w1.rearrange("(p j) c -> p j c", j=PACK)
+        w_half = [keep.tile([P, PACK, N // 2], F32, name="w_half%d" % h) for h in range(2)]
+        for h in range(2):
+            nc.sync.dma_start(w_half[h][:], w_rows[:, :, h * (N // 2) : (h + 1) * (N // 2)])
+
+        picked = keep.tile([P, PACK, HALF], BF16, name="picked")
+        x_grouped = keep.tile([P, S, PACK], BF16, name="x_grouped", align_bytes=64)
+        for j in range(PACK):
+            nc.vector.tensor_copy(x_grouped[:, 0:HALF, j], x_plane[j][:].indirect(offsets[:, 0 : HALF // 16]))
+            nc.scalar.activation(picked[:, j, :], x_plane[j][:].indirect(offsets[:, HALF // 16 : S // 16]), ACT.Copy)
+            if j % 2 == 1:
+                nc.vector.tensor_copy(
+                    out=x_grouped[:, HALF:S, j - 1 : j + 1].rearrange("p (c i) j -> p c j i", i=RUN),
+                    in_=picked[:, j - 1 : j + 1, :].rearrange("p j (c i) -> p c j i", i=RUN),
+                )
+        x_codes = keep.tile([P, S], U32, name="x_codes", align_bytes=64)
+        x_scales = keep.tile([P, S], U8, name="x_scales", align_bytes=64)
+        nc.vector.quantize_mx(out=x_codes[:].bitcast(FP8X4), scales=x_scales[:], in_=x_grouped[:].rearrange("p c j -> p (c j)"))
+
+        w_grouped = keep.tile([P, PACK, P, PACK], BF16, name="w_grouped", align_bytes=64)
+        w_dst = w_grouped[:].rearrange("p t m j -> p m j t")
+        w_src = [w_half[h][:].rearrange("p j (m t) -> p m j t", t=PACK) for h in range(2)]
+        nc.scalar.copy(out=w_dst[:, 0:64], in_=w_src[0])
+        nc.vector.tensor_copy(out=w_dst[:, 64 : 64 + W_SPLIT], in_=w_src[1][:, 0:W_SPLIT])
+        nc.scalar.copy(out=w_dst[:, 64 + W_SPLIT : P], in_=w_src[1][:, W_SPLIT:64])
+
+        w_codes = keep.tile([P, PACK, P], U32, name="w_codes", align_bytes=64)
+        w_scales = keep.tile([P, PACK, P], U8, name="w_scales", align_bytes=64)
+        for t in range(PACK):
+            nc.vector.quantize_mx(
+                out=w_codes[:, t, :].bitcast(FP8X4), scales=w_scales[:, t, :], in_=w_grouped[:, t].rearrange("p m j -> p (m j)")
+            )
+
+        scores = [psum.tile([P, S], F32, name="scores%d" % t) for t in range(PACK)]
+        neg_top = [keep.tile([P, 1], F32, name="neg_top%d" % t) for t in range(PACK)]
+        for t in range(PACK):
+            nc.tensor.matmul_mx(
+                out=scores[t][:],
+                lhsT=w_codes[:, t, :].bitcast(FP8X4),
+                lhsT_scale=w_scales[:, t, :],
+                rhs=x_codes[:].bitcast(FP8X4),
+                rhs_scale=x_scales[:],
+                start=True,
+                stop=True,
+            )
+            nc.vector.tensor_reduce(out=neg_top[t][:], in_=scores[t][:], axis=AXIS.X, op=ALU.max, negate=True)
+
+        exps = [keep.tile([P, S], F32, name="exps%d" % t) for t in range(PACK)]
+        total = [keep.tile([P, 1], F32, name="total%d" % t) for t in range(PACK)]
+        inverse = [keep.tile([P, 1], F32, name="inverse%d" % t) for t in range(PACK)]
+        for t in range(PACK):
+            nc.scalar.activation(out=exps[t][:], in_=scores[t][:], func=ACT.Exp, bias=neg_top[t][:], accum_out=total[t][:])
+
+        probs = keep.tile([P, PACK, S], F32, name="probs")
+        out_rows = out_0.rearrange("(p t) c -> p t c", t=PACK)
+        last = PACK - 1
+        for t in range(PACK):
+            nc.vector.reciprocal(out=inverse[t][:], in_=total[t][:])
+            pieces = [(0, S)] if t < last else [(O_SPLIT, S), (0, HALF), (HALF, O_SPLIT)]
+            for lo, hi in pieces:
+                nc.vector.tensor_scalar(out=probs[:, t, lo:hi], in0=exps[t][:, lo:hi], scalar1=inverse[t][:], scalar2=None, op0=ALU.mult)
+            nc.sync.dma_start(out_rows[:, t, :], probs[:, t, :])
+
+        p_grouped = keep.tile([P, S, PACK], BF16, name="p_grouped", align_bytes=64)
+        p_dst = p_grouped[:].rearrange("p (c i) t -> p c t i", i=RUN)
+        p_src = probs[:].rearrange("p t (c i) -> p c t i", i=RUN)
+        nc.scalar.copy(out=p_dst[:, O_SPLIT // RUN :], in_=p_src[:, O_SPLIT // RUN :])
+        nc.vector.tensor_copy(out=p_dst[:, 0 : HALF // RUN], in_=p_src[:, 0 : HALF // RUN])
+        nc.vector.tensor_copy(out=p_dst[:, HALF // RUN : O_SPLIT // RUN], in_=p_src[:, HALF // RUN : O_SPLIT // RUN])
+
+        p_codes = keep.tile([P, S], U32, name="p_codes", align_bytes=64)
+        p_scales = keep.tile([P, S], U8, name="p_scales", align_bytes=64)
+        words = out_1[0].rearrange("p c r -> p (c r)").bitcast(I32)
+        for h in range(2):
+            cols = slice(h * HALF, (h + 1) * HALF)
+            nc.vector.quantize_mx(
+                out=p_codes[:, cols].bitcast(FP8X4), scales=p_scales[:, cols], in_=p_grouped[:, cols].rearrange("p c t -> p (c t)")
+            )
+            nc.sync.dma_start(words[:, cols], p_codes[:, cols].bitcast(I32))
+        for q in range(4):
+            queue = nc.scalar if q % 2 == 0 else nc.sync
+            queue.dma_start(out_2[0, 4 * q : 4 * q + 4, :].bitcast(I32), p_scales[32 * q : 32 * q + 4, :].bitcast(I32))

@@ -31,12 +31,16 @@ def tile_picked_rank_none_lo_kernel(tc, xT, w1, offs, out_0, out_1, out_2):
         psum = ctx.enter_context(tc.psum_pool(name="psum", bufs=1))
 
         offsets = keep.tile([P, S // 16], U16, name="offsets")
-        nc.sync.dma_start(offsets[:], offs)
 
+        warm = keep.tile([P, 2], F32, name="warm")
+        nc.vector.memset(warm[:, 0:1], 0.0)
+        nc.scalar.activation(out=warm[:, 1:2], in_=warm[:, 0:1], func=ACT.Exp)
         x_rows = xT.rearrange("(p j) c -> p j c", j=PACK)
         x_plane = [keep.tile([P, T], F32, name="x_plane%d" % j) for j in range(PACK)]
         for j in range(PACK):
             nc.sync.dma_start(x_plane[j][:], x_rows[:, j, :])
+            if j == 0:
+                nc.sync.dma_start(offsets[:], offs)
         w_rows = w1.rearrange("(p j) c -> p j c", j=PACK)
         w_half = [keep.tile([P, PACK, N // 2], F32, name="w_half%d" % h) for h in range(2)]
         for h in range(2):
@@ -57,17 +61,17 @@ def tile_picked_rank_none_lo_kernel(tc, xT, w1, offs, out_0, out_1, out_2):
         nc.vector.quantize_mx(out=x_codes[:].bitcast(FP8X4), scales=x_scales[:], in_=x_grouped[:].rearrange("p c j -> p (c j)"))
 
         w_grouped = keep.tile([P, PACK, P, PACK], BF16, name="w_grouped", align_bytes=64)
-        w_dst = w_grouped[:].rearrange("p t m j -> p m j t")
-        w_src = [w_half[h][:].rearrange("p j (m t) -> p m j t", t=PACK) for h in range(2)]
-        nc.scalar.copy(out=w_dst[:, 0:64], in_=w_src[0])
-        nc.vector.tensor_copy(out=w_dst[:, 64 : 64 + W_SPLIT], in_=w_src[1][:, 0:W_SPLIT])
-        nc.scalar.copy(out=w_dst[:, 64 + W_SPLIT : P], in_=w_src[1][:, W_SPLIT:64])
+        w_dst = w_grouped[:].rearrange("p (u e) m j -> p u m j e", e=2)
+        w_src = [w_half[h][:].rearrange("p j (m u e) -> p u m j e", u=2, e=2) for h in range(2)]
+        nc.scalar.copy(out=w_dst[:, :, 0:64], in_=w_src[0])
+        nc.vector.tensor_copy(out=w_dst[:, :, 64 : 64 + W_SPLIT], in_=w_src[1][:, :, 0:W_SPLIT])
+        nc.scalar.copy(out=w_dst[:, :, 64 + W_SPLIT : P], in_=w_src[1][:, :, W_SPLIT:64])
 
-        w_codes = keep.tile([P, PACK, P], U32, name="w_codes", align_bytes=64)
-        w_scales = keep.tile([P, PACK, P], U8, name="w_scales", align_bytes=64)
+        w_codes = [keep.tile([P, P], U32, name="w_codes%d" % t, align_bytes=64) for t in range(PACK)]
+        w_scales = [keep.tile([P, P], U8, name="w_scales%d" % t, align_bytes=64) for t in range(PACK)]
         for t in range(PACK):
             nc.vector.quantize_mx(
-                out=w_codes[:, t, :].bitcast(FP8X4), scales=w_scales[:, t, :], in_=w_grouped[:, t].rearrange("p m j -> p (m j)")
+                out=w_codes[t][:].bitcast(FP8X4), scales=w_scales[t][:], in_=w_grouped[:, t].rearrange("p m j -> p (m j)")
             )
 
         scores = [psum.tile([P, S], F32, name="scores%d" % t) for t in range(PACK)]
@@ -75,8 +79,8 @@ def tile_picked_rank_none_lo_kernel(tc, xT, w1, offs, out_0, out_1, out_2):
         for t in range(PACK):
             nc.tensor.matmul_mx(
                 out=scores[t][:],
-                lhsT=w_codes[:, t, :].bitcast(FP8X4),
-                lhsT_scale=w_scales[:, t, :],
+                lhsT=w_codes[t][:].bitcast(FP8X4),
+                lhsT_scale=w_scales[t][:],
                 rhs=x_codes[:].bitcast(FP8X4),
                 rhs_scale=x_scales[:],
                 start=True,
@@ -101,11 +105,11 @@ def tile_picked_rank_none_lo_kernel(tc, xT, w1, offs, out_0, out_1, out_2):
             nc.sync.dma_start(out_rows[:, t, :], probs[:, t, :])
 
         p_grouped = keep.tile([P, S, PACK], BF16, name="p_grouped", align_bytes=64)
-        p_dst = p_grouped[:].rearrange("p (c i) t -> p c t i", i=RUN)
-        p_src = probs[:].rearrange("p t (c i) -> p c t i", i=RUN)
-        nc.scalar.copy(out=p_dst[:, O_SPLIT // RUN :], in_=p_src[:, O_SPLIT // RUN :])
-        nc.vector.tensor_copy(out=p_dst[:, 0 : HALF // RUN], in_=p_src[:, 0 : HALF // RUN])
-        nc.vector.tensor_copy(out=p_dst[:, HALF // RUN : O_SPLIT // RUN], in_=p_src[:, HALF // RUN : O_SPLIT // RUN])
+        p_dst = p_grouped[:].rearrange("p (c i) t -> p c t i", i=2)
+        p_src = probs[:].rearrange("p t (c i) -> p c t i", i=2)
+        nc.scalar.copy(out=p_dst[:, O_SPLIT // 2 :], in_=p_src[:, O_SPLIT // 2 :])
+        nc.vector.tensor_copy(out=p_dst[:, 0 : HALF // 2], in_=p_src[:, 0 : HALF // 2])
+        nc.vector.tensor_copy(out=p_dst[:, HALF // 2 : O_SPLIT // 2], in_=p_src[:, HALF // 2 : O_SPLIT // 2])
 
         p_codes = keep.tile([P, S], U32, name="p_codes", align_bytes=64)
         p_scales = keep.tile([P, S], U8, name="p_scales", align_bytes=64)

@@ -60,18 +60,20 @@ def tile_picked_rank_none_lo_kernel(tc, xT, w1, offs, out_0, out_1, out_2):
         x_scales = keep.tile([P, S], U8, name="x_scales", align_bytes=64)
         nc.vector.quantize_mx(out=x_codes[:].bitcast(FP8X4), scales=x_scales[:], in_=x_grouped[:].rearrange("p c j -> p (c j)"))
 
-        w_grouped = keep.tile([P, PACK, P, PACK], BF16, name="w_grouped", align_bytes=64)
-        w_dst = w_grouped[:].rearrange("p (u e) m j -> p u m j e", e=2)
+        w_grouped = [keep.tile([P, 2, P, PACK], BF16, name="w_grouped%d" % u, align_bytes=64) for u in range(2)]
+        w_dst = [w_grouped[u][:].rearrange("p e m j -> p m j e") for u in range(2)]
         w_src = [w_half[h][:].rearrange("p j (m u e) -> p u m j e", u=2, e=2) for h in range(2)]
-        nc.scalar.copy(out=w_dst[:, :, 0:64], in_=w_src[0])
-        nc.vector.tensor_copy(out=w_dst[:, :, 64 : 64 + W_SPLIT], in_=w_src[1][:, :, 0:W_SPLIT])
-        nc.scalar.copy(out=w_dst[:, :, 64 + W_SPLIT : P], in_=w_src[1][:, :, W_SPLIT:64])
+        for u in range(2):
+            nc.scalar.copy(out=w_dst[u][:, 0:64], in_=w_src[0][:, u])
+        nc.vector.tensor_copy(out=w_dst[0][:, 64 : 64 + W_SPLIT], in_=w_src[1][:, 0, 0:W_SPLIT])
+        nc.scalar.copy(out=w_dst[0][:, 64 + W_SPLIT : P], in_=w_src[1][:, 0, W_SPLIT:64])
+        nc.scalar.copy(out=w_dst[1][:, 64:P], in_=w_src[1][:, 1])
 
         w_codes = [keep.tile([P, P], U32, name="w_codes%d" % t, align_bytes=64) for t in range(PACK)]
         w_scales = [keep.tile([P, P], U8, name="w_scales%d" % t, align_bytes=64) for t in range(PACK)]
         for t in range(PACK):
             nc.vector.quantize_mx(
-                out=w_codes[t][:].bitcast(FP8X4), scales=w_scales[t][:], in_=w_grouped[:, t].rearrange("p m j -> p (m j)")
+                out=w_codes[t][:].bitcast(FP8X4), scales=w_scales[t][:], in_=w_grouped[t // 2][:, t % 2].rearrange("p m j -> p (m j)")
             )
 
         scores = [psum.tile([P, S], F32, name="scores%d" % t) for t in range(PACK)]
@@ -100,8 +102,11 @@ def tile_picked_rank_none_lo_kernel(tc, xT, w1, offs, out_0, out_1, out_2):
         for t in range(PACK):
             nc.vector.reciprocal(out=inverse[t][:], in_=total[t][:])
             pieces = [(0, S)] if t < last else [(O_SPLIT, S), (0, HALF), (HALF, O_SPLIT)]
-            for lo, hi in pieces:
-                nc.vector.tensor_scalar(out=probs[:, t, lo:hi], in0=exps[t][:, lo:hi], scalar1=inverse[t][:], scalar2=None, op0=ALU.mult)
+            if t == last - 1:
+                nc.scalar.activation(out=probs[:, t, :], in_=exps[t][:], func=ACT.Copy, scale=inverse[t][:])
+            else:
+                for lo, hi in pieces:
+                    nc.vector.tensor_scalar(out=probs[:, t, lo:hi], in0=exps[t][:, lo:hi], scalar1=inverse[t][:], scalar2=None, op0=ALU.mult)
             nc.sync.dma_start(out_rows[:, t, :], probs[:, t, :])
 
         p_grouped = keep.tile([P, S, PACK], BF16, name="p_grouped", align_bytes=64)

@@ -101,9 +101,10 @@ def tile_picked_rank_none_lo_kernel(tc, xT, w1, offs, out_0, out_1, out_2):
         last = PACK - 1
         for t in range(PACK):
             nc.vector.reciprocal(out=inverse[t][:], in_=total[t][:])
-            pieces = [(0, S)] if t < last else [(O_SPLIT, S), (0, HALF), (HALF, O_SPLIT)]
+            pieces = [(0, S)] if t < last else [(0, HALF), (O_SPLIT, S), (HALF, O_SPLIT)]
             if t == last - 1:
-                nc.scalar.activation(out=probs[:, t, :], in_=exps[t][:], func=ACT.Copy, scale=inverse[t][:])
+                nc.scalar.activation(out=probs[:, t, 0:O_SPLIT], in_=exps[t][:, 0:O_SPLIT], func=ACT.Copy, scale=inverse[t][:])
+                nc.scalar.activation(out=probs[:, t, O_SPLIT:S], in_=exps[t][:, O_SPLIT:S], func=ACT.Copy, scale=inverse[t][:])
             else:
                 for lo, hi in pieces:
                     nc.vector.tensor_scalar(out=probs[:, t, lo:hi], in0=exps[t][:, lo:hi], scalar1=inverse[t][:], scalar2=None, op0=ALU.mult)

from contextlib import ExitStack

import concourse.mybir as mybir

K, T, S, N = 512, 1024, 512, 512
FLOPS = 2 * K * S * N

F32 = mybir.dt.float32
BF16 = mybir.dt.bfloat16
I32 = mybir.dt.int32
U32 = mybir.dt.uint32
U16 = mybir.dt.uint16
U8 = mybir.dt.uint8
FP8X4 = mybir.dt.float8_e4m3fn_x4
ACT = mybir.ActivationFunctionType
ALU = mybir.AluOpType
AXIS = mybir.AxisListType

P = 128
PACK = 4
RUN = 4
HALF = S // 2
W_SPLIT = 44
O_SPLIT = 336


def tile_picked_rank_none_lo_kernel(tc, xT, w1, offs, out_0, out_1, out_2):
    nc = tc.nc
    with ExitStack() as ctx:
        keep = ctx.enter_context(tc.tile_pool(name="keep", bufs=1))
        psum = ctx.enter_context(tc.psum_pool(name="psum", bufs=1))

        offsets = keep.tile([P, S // 16], U16, name="offsets")

        warm = keep.tile([P, 2], F32, name="warm")
        nc.vector.memset(warm[:, 0:1], 0.0)
        nc.scalar.activation(out=warm[:, 1:2], in_=warm[:, 0:1], func=ACT.Exp)
        x_rows = xT.rearrange("(p j) c -> p j c", j=PACK)
        x_plane = [keep.tile([P, T], F32, name="x_plane%d" % j) for j in range(PACK)]
        for j in range(PACK):
            nc.sync.dma_start(x_plane[j][:], x_rows[:, j, :])
            if j == 0:
                nc.sync.dma_start(offsets[:], offs)
        w_rows = w1.rearrange("(p j) c -> p j c", j=PACK)
        w_half = [keep.tile([P, PACK, N // 2], F32, name="w_half%d" % h) for h in range(2)]
        for h in range(2):
            nc.sync.dma_start(w_half[h][:], w_rows[:, :, h * (N // 2) : (h + 1) * (N // 2)])

        picked = keep.tile([P, PACK, HALF], BF16, name="picked")
        x_grouped = keep.tile([P, S, PACK], BF16, name="x_grouped", align_bytes=64)
        for j in range(PACK):
            nc.vector.tensor_copy(x_grouped[:, 0:HALF, j], x_plane[j][:].indirect(offsets[:, 0 : HALF // 16]))
            nc.scalar.activation(picked[:, j, :], x_plane[j][:].indirect(offsets[:, HALF // 16 : S // 16]), ACT.Copy)
            if j % 2 == 1:
                nc.vector.tensor_copy(
                    out=x_grouped[:, HALF:S, j - 1 : j + 1].rearrange("p (c i) j -> p c j i", i=RUN),
                    in_=picked[:, j - 1 : j + 1, :].rearrange("p j (c i) -> p c j i", i=RUN),
                )
        x_codes = keep.tile([P, S], U32, name="x_codes", align_bytes=64)
        x_scales = keep.tile([P, S], U8, name="x_scales", align_bytes=64)
        nc.vector.quantize_mx(out=x_codes[:].bitcast(FP8X4), scales=x_scales[:], in_=x_grouped[:].rearrange("p c j -> p (c j)"))

        w_grouped = [keep.tile([P, 2, P, PACK], BF16, name="w_grouped%d" % u, align_bytes=64) for u in range(2)]
        w_dst = [w_grouped[u][:].rearrange("p e m j -> p m j e") for u in range(2)]
        w_src = [w_half[h][:].rearrange("p j (m u e) -> p u m j e", u=2, e=2) for h in range(2)]
        for u in range(2):
            nc.scalar.copy(out=w_dst[u][:, 0:64], in_=w_src[0][:, u])
        nc.vector.tensor_copy(out=w_dst[0][:, 64 : 64 + W_SPLIT], in_=w_src[1][:, 0, 0:W_SPLIT])
        nc.scalar.copy(out=w_dst[0][:, 64 + W_SPLIT : P], in_=w_src[1][:, 0, W_SPLIT:64])
        nc.scalar.copy(out=w_dst[1][:, 64:P], in_=w_src[1][:, 1])

        w_codes = [keep.tile([P, P], U32, name="w_codes%d" % t, align_bytes=64) for t in range(PACK)]
        w_scales = [keep.tile([P, P], U8, name="w_scales%d" % t, align_bytes=64) for t in range(PACK)]
        for t in range(PACK):
            nc.vector.quantize_mx(
                out=w_codes[t][:].bitcast(FP8X4), scales=w_scales[t][:], in_=w_grouped[t // 2][:, t % 2].rearrange("p m j -> p (m j)")
            )

        scores = [psum.tile([P, S], F32, name="scores%d" % t) for t in range(PACK)]
        neg_top = [keep.tile([P, 1], F32, name="neg_top%d" % t) for t in range(PACK)]
        for t in range(PACK):
            nc.tensor.matmul_mx(
                out=scores[t][:],
                lhsT=w_codes[t][:].bitcast(FP8X4),
                lhsT_scale=w_scales[t][:],
                rhs=x_codes[:].bitcast(FP8X4),
                rhs_scale=x_scales[:],
                start=True,
                stop=True,
            )
            nc.vector.tensor_reduce(out=neg_top[t][:], in_=scores[t][:], axis=AXIS.X, op=ALU.max, negate=True)

        exps = [keep.tile([P, S], F32, name="exps%d" % t) for t in range(PACK)]
        total = [keep.tile([P, 1], F32, name="total%d" % t) for t in range(PACK)]
        inverse = [keep.tile([P, 1], F32, name="inverse%d" % t) for t in range(PACK)]
        for t in range(PACK):
            nc.scalar.activation(out=exps[t][:], in_=scores[t][:], func=ACT.Exp, bias=neg_top[t][:], accum_out=total[t][:])

        probs = keep.tile([P, PACK, S], F32, name="probs")
        out_rows = out_0.rearrange("(p t) c -> p t c", t=PACK)
        last = PACK - 1
        for t in range(PACK):
            nc.vector.reciprocal(out=inverse[t][:], in_=total[t][:])
            pieces = [(0, S)] if t < last else [(0, HALF), (O_SPLIT, S), (HALF, O_SPLIT)]
            if t == last - 1:
                nc.scalar.activation(out=probs[:, t, 0:O_SPLIT], in_=exps[t][:, 0:O_SPLIT], func=ACT.Copy, scale=inverse[t][:])
                nc.scalar.activation(out=probs[:, t, O_SPLIT:S], in_=exps[t][:, O_SPLIT:S], func=ACT.Copy, scale=inverse[t][:])
            else:
                for lo, hi in pieces:
                    nc.vector.tensor_scalar(out=probs[:, t, lo:hi], in0=exps[t][:, lo:hi], scalar1=inverse[t][:], scalar2=None, op0=ALU.mult)
            nc.sync.dma_start(out_rows[:, t, :], probs[:, t, :])

        p_grouped = keep.tile([P, S, PACK], BF16, name="p_grouped", align_bytes=64)
        p_dst = p_grouped[:].rearrange("p (c i) t -> p c t i", i=2)
        p_src = probs[:].rearrange("p t (c i) -> p c t i", i=2)
        nc.scalar.copy(out=p_dst[:, O_SPLIT // 2 :], in_=p_src[:, O_SPLIT // 2 :])
        nc.vector.tensor_copy(out=p_dst[:, 0 : HALF // 2], in_=p_src[:, 0 : HALF // 2])
        nc.vector.tensor_copy(out=p_dst[:, HALF // 2 : O_SPLIT // 2], in_=p_src[:, HALF // 2 : O_SPLIT // 2])

        p_codes = keep.tile([P, S], U32, name="p_codes", align_bytes=64)
        p_scales = keep.tile([P, S], U8, name="p_scales", align_bytes=64)
        words = out_1[0].rearrange("p c r -> p (c r)").bitcast(I32)
        for h in range(2):
            cols = slice(h * HALF, (h + 1) * HALF)
            nc.vector.quantize_mx(
                out=p_codes[:, cols].bitcast(FP8X4), scales=p_scales[:, cols], in_=p_grouped[:, cols].rearrange("p c t -> p (c t)")
            )
            nc.sync.dma_start(words[:, cols], p_codes[:, cols].bitcast(I32))
        for q in range(4):
            queue = nc.scalar if q % 2 == 0 else nc.sync
            queue.dma_start(out_2[0, 4 * q : 4 * q + 4, :].bitcast(I32), p_scales[32 * q : 32 * q + 4, :].bitcast(I32))
